import numpy as np, ml_dtypes
CORES = [10,34,74,98]
N = 4
import mx_ref
BF = ml_dtypes.bfloat16
def entries(a):
    return np.ascontiguousarray(a.T).reshape(-1)
def table(e):
    return np.ascontiguousarray(np.reshape(e, (-1, 16)).T).astype(np.int32)
def cols(t, e):
    v = np.concatenate([t.reshape(128, -1, 4), np.zeros((128, 1, 4), BF)], axis=1)
    return np.ascontiguousarray(v[:, e]).reshape(128, -1)
def f(rng, *shape):
    return mx_ref.flush((rng.standard_normal(shape, dtype=np.float32) * np.exp2(rng.integers(-2, 3, shape[:-1] + (1,)))).astype(BF))
def wide(rng, *shape, cols=0):
    v = rng.standard_normal(shape, dtype=np.float32) * np.exp2(rng.integers(-12, 13, shape)).astype(np.float32)
    if cols: v *= np.repeat(np.exp2(rng.integers(-cols, cols + 1, shape[:-2] + (1, shape[-1] // 4))) * (rng.random(shape[:-2] + (1, shape[-1] // 4)) > 0.0625), 4, axis=-1).astype(np.float32)
    return mx_ref.flush(v.astype(BF))
T, CAPP = 512, 192
def lists(rng, full=False, skew=False, single=False, back=False):
    if full:
        v = rng.permutation(([CAPP] * (T // CAPP) + [T % CAPP] + [0] * N)[:N])
        n = v[(np.arange(N)[None, :] - np.arange(N)[:, None]) % N][rng.permutation(N)][:, rng.permutation(N)]
    else:
        n = np.full((N, N), T // N)
        for _ in range(20 * N):
            (s, t), (d, e) = rng.permutation(N)[:2], rng.permutation(N)[:2]
            k = rng.integers(0, min(n[s, d], n[t, e], CAPP - n[s, e], CAPP - n[t, d]) + 1)
            n[s, d] -= k; n[t, e] -= k; n[s, e] += k; n[t, d] += k
    a = np.full((N, N * CAPP), -1)
    for s in range(N):
        parts = np.split(rng.permutation(T), np.cumsum(n[s])[:-1])
        for d in range(N): a[s, d * CAPP + rng.permutation(CAPP)[:n[s, d]]] = parts[d]
    p, u, o = [], [], []
    for r in range(N):
        used = np.flatnonzero(a[:, r * CAPP:(r + 1) * CAPP].reshape(-1) >= 0)
        p.append(table(used[::-1] if back else rng.permutation(used)))
        h = rng.integers(0, N)
        c = rng.integers(0, 2, N) if full else (np.full(N, -1) if rng.random() < 0.5 else rng.integers(0, 2, N)) if single else rng.integers(-1, 2, N)
        if c[h] < 0: c[h] = rng.integers(0, 2)
        named = np.flatnonzero(c >= 0)
        if single: named = np.array([h])
        if skew:
            m = rng.integers(T // 2 + 1, T + 1)
            e = np.sort(np.concatenate([np.full(m, h), rng.choice(named, T - m)]))
        elif full: e = np.sort(np.concatenate([named, rng.choice(named, T - N)]))
        else: e = np.repeat(named, np.diff(np.concatenate([[0], np.sort(rng.integers(0, T + 1, len(named) - 1)), [T]])))
        u.append(table(np.concatenate([c, np.full(16 - N, -1)]))); o.append(table(e))
    return {"send": np.stack([table(k) for k in a]), "place": np.stack(p), "sel": np.stack(u), "of": np.stack(o)}
def setup_inputs(rng):
    return {"x": f(rng, N, 128, 4 * T), "w": f(rng, N, 256, 512), **lists(rng)}
def setup_inputs_full(rng):
    return {**setup_inputs(rng), **lists(rng, full=True)}
def setup_inputs_reversed(rng):
    return {**setup_inputs(rng), **lists(rng, back=True)}
def setup_inputs_single(rng):
    return {**setup_inputs(rng), **lists(rng, single=True)}
def setup_inputs_skew(rng):
    return {**setup_inputs(rng), **lists(rng, skew=True)}
def setup_inputs_spread(rng):
    d = setup_inputs(rng); d["x"] = wide(rng, N, 128, 4 * T, cols=8); return d
def check_inputs(d):
    b = []
    for k in ("x", "w"):
        a = np.abs(d[k].astype(np.float32))
        if not ((a == 0) | ((a >= 2.0 ** -30) & (a <= 2.0 ** 30))).all(): b.append(k)
    sends = np.stack([entries(d["send"][r]) for r in range(N)])
    for r in range(N):
        c, p, u, e = sends[r], entries(d["place"][r]), entries(d["sel"][r]), entries(d["of"][r])
        if c.min() < -1 or not np.array_equal(np.sort(c[c >= 0]), np.arange(T)): b.append("send")
        if not np.array_equal(np.sort(p), np.flatnonzero(sends[:, r * CAPP:(r + 1) * CAPP].reshape(-1) >= 0)): b.append("place")
        if u.min() < -1 or u.max() > 1 or (u[N:] != -1).any(): b.append("sel")
        if e.min() < 0 or e.max() >= N or (np.diff(e) < 0).any() or (u[e] < 0).any(): b.append("of")
    return b
def reference(x, w, send, place, sel, of):
    W = [[mx_ref.quantize(w[h][128 * m:128 * m + 128]) for m in range(2)] for h in range(N)]
    y = np.zeros((N, 128, T), np.float32)
    for r in range(N):
        slots = np.concatenate([cols(x[s], entries(send[s])[r * CAPP:(r + 1) * CAPP]) for s in range(N)], axis=1)
        X = mx_ref.quantize(cols(slots, entries(place[r])))
        u, e = entries(sel[r]), entries(of[r])
        for h in range(N):
            i = e == h
            if i.any(): y[r][:, i] = mx_ref.matmul(W[h][u[h]], X)[:, i]
    return {"y": y}

@@ -1,0 +1,266 @@
+from concourse.bass import DstId, RemoteDMATransfer
+from concourse.mybir import dt, AluOpType, ActivationFunctionType
+
+N, COLS, CAP, F = 4, 512, 192, 128
+PAIR = 2 * CAP
+ALL = N * CAP
+EXPERTS = 6
+CODES = "float8_e4m3fn_x4"
+
+SCRATCH = {
+    "xs": ("sbuf", [128, 4 * COLS], "bfloat16"),
+    "ws": ("sbuf", [128, 8 * F], "bfloat16"),
+    "slist": ("sbuf", [128, N * CAP // 16], "int32"),
+    "seli": ("sbuf", [128, 16], "int32"),
+    "po": ("sbuf", [16, 64], "int32"),
+    "ip": ("sbuf", [128, 32], "int32"),
+    "ia": ("sbuf", [128, 32], "int32"),
+    "ic": ("sbuf", [128, 32], "int32"),
+    "jj": ("sbuf", [128, 32], "float32"),
+    "self_": ("sbuf", [128, 16], "float32"),
+    "selb": ("sbuf", [128, 4], "float32"),
+    "selin": ("sbuf", [128, 4], "float32"),
+    "ox": ("sbuf", [128, N * CAP // 16], "uint16"),
+    "oe": ("sbuf", [128, 64], "uint16"),
+    "base": ("sbuf", [16, 2], "float32"),
+    "oa": ("sbuf", [16, 128], "float32"),
+    "ob": ("sbuf", [16, 128], "float32"),
+    "off1": ("sbuf", [16, 32], "uint16"),
+    "off": ("sbuf", [128, 32], "uint16"),
+    "xtq": ("sbuf", [128, 4 * PAIR], "bfloat16"),
+    "xtp": ("sbuf", [128, 4 * CAP], "bfloat16"),
+    "xto": ("sbuf", [128, 4 * CAP], "bfloat16"),
+    "et": ("sbuf", [128, 8 * F], "bfloat16"),
+    "eco": ("sbuf", [128, 2 * F], CODES),
+    "xcp": ("sbuf", [128, CAP], CODES),
+    "spp": ("sbuf", [128, CAP + 2 * F], "uint8"),
+    "xcq": ("sbuf", [128, PAIR], CODES),
+    "ecq": ("sbuf", [128, 2 * F], CODES),
+    "sql": ("sbuf", [128, CAP + F], "uint8"),
+    "sqh": ("sbuf", [128, CAP + F], "uint8"),
+    "xc1": ("sbuf", [128, PAIR], CODES),
+    "epc": ("sbuf", [128, 2 * F], CODES),
+    "sc1": ("sbuf", [128, PAIR + 2 * F], "uint8"),
+    "xc2": ("sbuf", [128, PAIR], CODES),
+    "eqc": ("sbuf", [128, 2 * F], CODES),
+    "sc2": ("sbuf", [128, PAIR + 2 * F], "uint8"),
+    "hx": ("sbuf", [128, CAP], CODES),
+    "ps": ("psum", [128, 4096], "float32"),
+    "res": ("sbuf", [128, EXPERTS * ALL], "float32"),
+    "yb": ("sbuf", [128, COLS], "float32"),
+}
+SEMAPHORES = ["l_sel", "l_list", "l_w", "l_x", "l_po", "l_off",
+              "e_i1", "e_i2", "e_ia", "e_j", "e_self", "e_selb", "e_ox", "e_E",
+              "e_gq", "e_xq", "e_gp", "e_xp", "e_oe", "e_ge", "e_e", "e_go", "e_xo",
+              "e_base", "e_m", "e_s1", "e_s2", "e_s3", "e_off",
+              "selarr", "parr", "eql", "eqh", "xq", "hin", "sent",
+              "e_yv", "e_ys", "st"] + ["mm%d" % k for k in range(12)] + ["cp%d" % k for k in range(12)]
+
+
+def u8(view):
+    return view.bitcast(dt.uint8)
+
+
+def bits(engines):
+    return sum(1 << e for e in engines)
+
+
+def helpers(r, T, topo):
+    c = T.cores[r]
+    l = 2 * (1 - r // 2)
+    other = [k for k in topo.cores_of(c) if topo.die(k) != topo.die(c)]
+    out = {}
+    for d in sorted((l, l + 1), key=lambda d: sum(topo.may_write(k, T.cores[d]) for k in other)):
+        k = [k for k in other if topo.may_write(k, T.cores[d]) and k not in out.values()][0]
+        out[d] = k
+    return out
+
+
+def hand_on(g, core, T, topo, s, d):
+    dst = T.cores[d]
+    rid, pid, _ = topo.addr(dst)
+    n = len(topo.engines(core, dst))
+    a = (s % 2) * CAP
+    g.wait_ge(T.sem.hin, 8)
+    g.remote_dma(u8(T.xc2[:, a:a + CAP]), u8(T.hx[:]), T.sem.xq, T.sem.sent, pid, rid, topo.mask(core, dst))
+    g.wait_ge(T.sem.sent, n)
+
+
+def rank_program(g, core, T, topo):
+    r = T.rank_of(core)
+    if r is None:
+        for s in range(N):
+            for d, k in helpers(s, T, topo).items():
+                if k == core:
+                    hand_on(g, core, T, topo, s, d)
+        return
+    S, v, sc, te, sy = T.sem, g.vector, g.scalar, g.tensor, g.sync
+    A, COPY = AluOpType, ActivationFunctionType.Copy
+    p, l = r ^ 1, 2 * (1 - r // 2)
+    h = l + 1
+    odd = r % 2
+    dst = {d: T.cores[d] for d in (p, l, h)}
+    help_ = helpers(r, T, topo)
+    sent = [0]
+
+    def one(out, in_, sem, d, mask, n):
+        rid, pid, _ = topo.addr(d)
+        g.remote_dma(out, in_, sem, S.sent, pid, rid, mask)
+        sent[0] += n
+
+    def two(items):
+        tr = []
+        for i, (out, in_, sem, d) in enumerate(items):
+            en = topo.engines(core, d)
+            half = en[:len(en) // 2] if i == 0 else en[len(en) // 2:]
+            rid, pid, _ = topo.addr(d)
+            tr.append(RemoteDMATransfer(dst_ids=[DstId(rid=rid, pnc=pid)], dma_engine_mask=bits(half), remote_sem=sem, src=in_, dst=out))
+            sent[0] += len(half)
+        g.remote_dma_fused(tr, local_sem=S.sent)
+
+    spp_e, spp_x = (CAP, 0) if odd else (0, 2 * F)
+    sq_e, sq_x = (CAP, 0) if odd else (0, F)
+    if odd:
+        sc1_e, sc1_x, own = 0, 2 * F, CAP
+    else:
+        sc1_e, sc1_x, own = PAIR, 0, 0
+    land_p = CAP if odd else 0
+    land_sp = CAP if odd else 0
+    land_sq = (CAP + F) if odd else 0
+    land_e = F if odd else 0
+
+    sc.dma_start(T.seli[0:1, 0:16], T.sel[:]).then_inc(S.l_sel, 16)
+    for k in range(4):
+        sc.dma_start(T.slist[16 * k:16 * k + 16, :], T.send[:]).then_inc(S.l_list, 16)
+    sc.dma_start(T.xs[:], T.x[:]).then_inc(S.l_x, 16)
+    sy.dma_start(T.ws[:, 0:512], T.w[0:128, :]).then_inc(S.l_w, 16)
+    sy.dma_start(T.ws[:, 512:1024], T.w[128:256, :]).then_inc(S.l_w, 16)
+    for k in range(4, 8):
+        sy.dma_start(T.slist[16 * k:16 * k + 16, :], T.send[:]).then_inc(S.l_list, 16)
+    sy.dma_start(T.po[:, 0:32], T.place[:]).then_inc(S.l_po, 16)
+    sy.dma_start(T.po[:, 32:64], T.of[:]).then_inc(S.l_po, 16)
+
+    g.iota(T.ip[:], [[0, 32]], 0, 1).then_inc(S.e_i1, 1)
+    g.iota(T.ic[:], [[16, 32]], 0, 0).then_inc(S.e_i2, 1)
+    g.wait_ge(S.e_self, 1)
+    g.partition_broadcast(T.selb[:, 0:4], T.self_[0:1, 0:4], 128).then_inc(S.e_selb, 1)
+    g.wait_ge(S.e_selb, 1)
+    two([(T.selin[:, odd:odd + 1], T.selb[:, d:d + 1], S.selarr, dst[d]) for d in (l, h)])
+    m = topo.mask(core, dst[p])
+    n = len(topo.engines(core, dst[p]))
+    g.wait_ge(S.e_E, 1)
+    one(u8(T.epc[:]), u8(T.eco[:]), S.parr, dst[p], m, n)
+    g.wait_ge(S.e_xq, 2)
+    two([(u8(T.hx[:]), u8(T.xcq[:, i * CAP:(i + 1) * CAP]), S.hin, help_[d]) for i, d in enumerate((l, h))])
+    g.wait_ge(S.e_xp, 1)
+    one(u8(T.xc1[:, land_p:land_p + CAP]), u8(T.xcp[:]), S.parr, dst[p], m, n)
+    one(T.sc1[:, land_sp:land_sp + CAP + 2 * F], T.spp[:], S.parr, dst[p], m, n)
+    g.wait_ge(S.e_e, 2)
+    esem = S.eqh if odd else S.eql
+    two([(u8(T.eqc[:, land_e:land_e + F]), u8(T.ecq[:, i * F:(i + 1) * F]), esem, dst[d]) for i, d in enumerate((l, h))])
+    two([(T.sc2[:, land_sq:land_sq + CAP + F], q[:], esem, dst[d]) for q, d in ((T.sql, l), (T.sqh, h))])
+    g.wait_ge(S.sent, sent[0])
+
+    v.wait_ge(S.e_i1, 1)
+    v.tensor_scalar(T.ia[:], T.ip[:], 15, None, A.bitwise_and).then_inc(S.e_ia, 1)
+    v.wait_ge(S.e_i2, 1)
+    v.wait_ge(S.e_ia, 1)
+    v.tensor_tensor(T.jj[:], T.ia[:], T.ic[:], A.add).then_inc(S.e_j, 1)
+    v.wait_ge(S.l_sel, 16)
+    v.tensor_scalar(T.self_[0:1, :], T.seli[0:1, :], 512.0, 0.0, A.mult, A.max).then_inc(S.e_self, 1)
+    v.wait_ge(S.l_list, 128)
+    v.tensor_scalar(T.ox[:], T.slist[:], 4.0, 0.0, A.mult, A.max).then_inc(S.e_ox, 1)
+    v.wait_ge(S.l_w, 32)
+    v.quantize_mx(T.eco[:], T.spp[:, spp_e:spp_e + 2 * F], T.ws[:]).then_inc(S.e_E, 1)
+
+    def gather(tile, n, first, sem):
+        o = T.ox[:, first // 16:(first + n) // 16]
+        for t in range(2):
+            v.tensor_copy(tile[:, t:4 * n:4], T.xs[:, t:4 * COLS].indirect(o)).then_inc(sem, 1)
+        for t in range(2, 4):
+            sc.activation(tile[:, t:4 * n:4], T.xs[:, t:4 * COLS].indirect(o), COPY).then_inc(sem, 1)
+        v.wait_ge(sem, 4)
+
+    for q in (v, sc):
+        q.wait_ge(S.l_x, 16)
+        q.wait_ge(S.e_ox, 1)
+    gather(T.xtq, PAIR, l * CAP, S.e_gq)
+    for i, q in enumerate((T.sql, T.sqh)):
+        v.quantize_mx(T.xcq[:, i * CAP:(i + 1) * CAP], q[:, sq_x:sq_x + CAP], T.xtq[:, 4 * i * CAP:4 * (i + 1) * CAP]).then_inc(S.e_xq, 1)
+    gather(T.xtp, CAP, p * CAP, S.e_gp)
+    v.quantize_mx(T.xcp[:], T.spp[:, spp_x:spp_x + CAP], T.xtp[:]).then_inc(S.e_xp, 1)
+    v.wait_ge(S.selarr, 8)
+    v.wait_ge(S.e_j, 1)
+    for i in range(2):
+        v.tensor_scalar(T.oe[:, 32 * i:32 * i + 32], T.jj[:], T.selin[:, i:i + 1], None, A.add).then_inc(S.e_oe, 1)
+    for q in (v, sc):
+        q.wait_ge(S.e_oe, 2)
+    sc.wait_ge(S.l_w, 32)
+    v.tensor_copy(T.et[:, 0:512], T.ws[:, 0:1024].indirect(T.oe[:, 0:32])).then_inc(S.e_ge, 1)
+    sc.activation(T.et[:, 512:1024], T.ws[:, 0:1024].indirect(T.oe[:, 32:64]), COPY).then_inc(S.e_ge, 1)
+    v.wait_ge(S.e_ge, 2)
+    for i, q in enumerate((T.sql, T.sqh)):
+        v.quantize_mx(T.ecq[:, i * F:(i + 1) * F], q[:, sq_e:sq_e + F], T.et[:, 512 * i:512 * (i + 1)]).then_inc(S.e_e, 1)
+    gather(T.xto, CAP, r * CAP, S.e_go)
+    so = sc1_x + own
+    v.quantize_mx(T.xc1[:, own:own + CAP], T.sc1[:, so:so + CAP], T.xto[:]).then_inc(S.e_xo, 1)
+    v.wait_ge(S.l_po, 32)
+    v.wait_ge(S.e_selb, 1)
+    v.tensor_scalar(T.base[:, 0:1], T.selb[0:16, r:r + 1], ALL / 512.0, None, A.mult).then_inc(S.e_base, 1)
+    v.tensor_scalar(T.base[:, 1:2], T.selb[0:16, p:p + 1], ALL / 512.0, 2.0 * ALL, A.mult, A.add).then_inc(S.e_base, 1)
+    v.wait_ge(S.e_base, 2)
+    of, place = T.po[:, 32:64], T.po[:, 0:32]
+    for i, (who, b) in enumerate(((r, T.base[:, 0:1]), (p, T.base[:, 1:2]), (l, 4.0 * ALL), (h, 5.0 * ALL))):
+        v.tensor_scalar(T.oa[:, 32 * i:32 * i + 32], of, float(who), b, A.is_equal, A.mult).then_inc(S.e_m, 1)
+    v.wait_ge(S.e_m, 4)
+    v.tensor_tensor(T.ob[:, 0:64], T.oa[:, 0:64], T.oa[:, 64:128], A.add).then_inc(S.e_s1, 1)
+    v.wait_ge(S.e_s1, 1)
+    v.tensor_tensor(T.ob[:, 64:96], T.ob[:, 0:32], T.ob[:, 32:64], A.add).then_inc(S.e_s2, 1)
+    v.wait_ge(S.e_s2, 1)
+    v.tensor_tensor(T.ob[:, 96:128], T.ob[:, 64:96], place, A.add).then_inc(S.e_s3, 1)
+    v.wait_ge(S.e_s3, 1)
+    v.tensor_copy(T.off1[:], T.ob[:, 96:128]).then_inc(S.e_off, 1)
+    sy.wait_ge(S.e_off, 1)
+    for k in range(8):
+        sy.dma_start(T.off[16 * k:16 * k + 16, :], T.off1[:]).then_inc(S.l_off, 16)
+
+    def expert(e):
+        a = (e % 2) * F
+        if e < 2:
+            return T.eco[:, a:a + F], T.spp[:, spp_e + a:spp_e + a + F]
+        if e < 4:
+            return T.epc[:, a:a + F], T.sc1[:, sc1_e + a:sc1_e + a + F]
+        b = 0 if e == 4 else F + PAIR
+        return T.eqc[:, a:a + F], T.sc2[:, b:b + F]
+    group = {0: (T.xc1[:], T.sc1[:, sc1_x:sc1_x + PAIR], r // 2), 1: (T.xc2[:], T.sc2[:, F:F + PAIR], 1 - r // 2)}
+    own_w, p_w, l_w, h_w, x_w = (S.e_E, 1), (S.parr, 3 * n), (S.eql, 8), (S.eqh, 8), (S.xq, 16)
+    order = [(0, 0, [own_w, p_w, (S.e_xo, 1)]), (1, 0, []), (2, 0, []), (3, 0, []),
+             (4, 0, [l_w]), (5, 0, [h_w]), (4, 1, [x_w]), (5, 1, []), (0, 1, []), (1, 1, []), (2, 1, []), (3, 1, [])]
+    for k, (e, gr, waits) in enumerate(order):
+        for sem, val in waits:
+            te.wait_ge(sem, val)
+        if k >= 8:
+            te.wait_ge(S["cp%d" % (k - 8)], 1)
+        bank = 512 * (k % 8)
+        W, Ws = expert(e)
+        X, Xs, pos = group[gr]
+        te.matmul_mx(T.ps[:, bank:bank + PAIR], W, Ws, X, Xs, True, True).then_inc(S["mm%d" % k], 1)
+        q = sc if k % 2 else v
+        q.wait_ge(S["mm%d" % k], 1)
+        o = T.res[:, e * ALL + pos * PAIR:e * ALL + (pos + 1) * PAIR]
+        if k % 2:
+            sc.activation(o, T.ps[:, bank:bank + PAIR], COPY).then_inc(S["cp%d" % k], 1)
+        else:
+            v.tensor_copy(o, T.ps[:, bank:bank + PAIR]).then_inc(S["cp%d" % k], 1)
+
+    for q in (v, sc):
+        q.wait_ge(S.l_off, 128)
+        for k in range(12):
+            q.wait_ge(S["cp%d" % k], 1)
+    v.tensor_copy(T.yb[:, 0:256], T.res[:].indirect(T.off[:, 0:16])).then_inc(S.e_yv, 1)
+    sc.activation(T.yb[:, 256:512], T.res[:].indirect(T.off[:, 16:32]), COPY).then_inc(S.e_ys, 1)
+    sy.wait_ge(S.e_yv, 1)
+    sy.dma_start(T.y[:, 0:256], T.yb[:, 0:256]).then_inc(S.st, 16)
+    sc.wait_ge(S.e_ys, 1)
+    sc.dma_start(T.y[:, 256:512], T.yb[:, 256:512]).then_inc(S.st, 16)
+    sy.wait_ge(S.st, 32)

@@ -1,60 +1,69 @@
-from concourse.bass import DstId, RemoteDMATransfer
+from concourse.bass import DstId, RemoteDMATransfer, IndirectOffsetOnAxis
 from concourse.mybir import dt, AluOpType, ActivationFunctionType
 
 N, COLS, CAP, F = 4, 512, 192, 128
+NCORES = 112
 PAIR = 2 * CAP
 ALL = N * CAP
-EXPERTS = 6
 CODES = "float8_e4m3fn_x4"
+ROLES = "MBD"
+OWN_BY_DMA = False
 
 SCRATCH = {
     "xs": ("sbuf", [128, 4 * COLS], "bfloat16"),
     "ws": ("sbuf", [128, 8 * F], "bfloat16"),
-    "slist": ("sbuf", [128, N * CAP // 16], "int32"),
+    "slist": ("sbuf", [32, ALL // 16], "int32"),
     "seli": ("sbuf", [128, 16], "int32"),
-    "po": ("sbuf", [16, 64], "int32"),
+    "po": ("sbuf", [32, 64], "int32"),
     "ip": ("sbuf", [128, 32], "int32"),
     "ia": ("sbuf", [128, 32], "int32"),
     "ic": ("sbuf", [128, 32], "int32"),
     "jj": ("sbuf", [128, 32], "float32"),
+    "pf": ("sbuf", [128, 4], "float32"),
+    "row": ("sbuf", [128, 4], "int32"),
     "self_": ("sbuf", [128, 16], "float32"),
     "selb": ("sbuf", [128, 4], "float32"),
     "selin": ("sbuf", [128, 4], "float32"),
-    "ox": ("sbuf", [128, N * CAP // 16], "uint16"),
-    "oe": ("sbuf", [128, 64], "uint16"),
-    "base": ("sbuf", [16, 2], "float32"),
-    "oa": ("sbuf", [16, 128], "float32"),
-    "ob": ("sbuf", [16, 128], "float32"),
-    "off1": ("sbuf", [16, 32], "uint16"),
+    "ox": ("sbuf", [128, ALL // 16], "uint16"),
+    "oe": ("sbuf", [128, 32 * N], "uint16"),
+    "oa": ("sbuf", [32, 32], "float32"),
+    "ob": ("sbuf", [32, 32], "float32"),
     "off": ("sbuf", [128, 32], "uint16"),
-    "xtq": ("sbuf", [128, 4 * PAIR], "bfloat16"),
-    "xtp": ("sbuf", [128, 4 * CAP], "bfloat16"),
-    "xto": ("sbuf", [128, 4 * CAP], "bfloat16"),
-    "et": ("sbuf", [128, 8 * F], "bfloat16"),
-    "eco": ("sbuf", [128, 2 * F], CODES),
-    "xcp": ("sbuf", [128, CAP], CODES),
-    "spp": ("sbuf", [128, CAP + 2 * F], "uint8"),
-    "xcq": ("sbuf", [128, PAIR], CODES),
-    "ecq": ("sbuf", [128, 2 * F], CODES),
-    "sql": ("sbuf", [128, CAP + F], "uint8"),
-    "sqh": ("sbuf", [128, CAP + F], "uint8"),
-    "xc1": ("sbuf", [128, PAIR], CODES),
-    "epc": ("sbuf", [128, 2 * F], CODES),
-    "sc1": ("sbuf", [128, PAIR + 2 * F], "uint8"),
-    "xc2": ("sbuf", [128, PAIR], CODES),
-    "eqc": ("sbuf", [128, 2 * F], CODES),
-    "sc2": ("sbuf", [128, PAIR + 2 * F], "uint8"),
-    "hx": ("sbuf", [128, CAP], CODES),
+    "xt": ("sbuf", [128, 4 * ALL], "bfloat16"),
+    "et": ("sbuf", [128, 4 * F * N], "bfloat16"),
+    "oxc": ("sbuf", [128, ALL], CODES),
+    "oxp": ("sbuf", [128, ALL], "uint8"),
+    "oec": ("sbuf", [128, N * F], CODES),
+    "oep": ("sbuf", [128, N * F], "uint8"),
+    "xc": ("sbuf", [128, ALL], CODES),
+    "xp": ("sbuf", [128, ALL], "uint8"),
+    "ec": ("sbuf", [128, N * F], CODES),
+    "ep": ("sbuf", [128, N * F], "uint8"),
     "ps": ("psum", [128, 4096], "float32"),
-    "res": ("sbuf", [128, EXPERTS * ALL], "float32"),
+    "res": ("sbuf", [128, N * ALL], "float32"),
     "yb": ("sbuf", [128, COLS], "float32"),
 }
-SEMAPHORES = ["l_sel", "l_list", "l_w", "l_x", "l_po", "l_off",
-              "e_i1", "e_i2", "e_ia", "e_j", "e_self", "e_selb", "e_ox", "e_E",
-              "e_gq", "e_xq", "e_gp", "e_xp", "e_oe", "e_ge", "e_e", "e_go", "e_xo",
-              "e_base", "e_m", "e_s1", "e_s2", "e_s3", "e_off",
-              "selarr", "parr", "eql", "eqh", "xq", "hin", "sent",
-              "e_yv", "e_ys", "st"] + ["mm%d" % k for k in range(12)] + ["cp%d" % k for k in range(12)]
+KINDS = ("sel", "xc", "xp", "ec", "ep")
+SEMAPHORES = (["l_sel", "l_list", "l_w", "l_x", "l_po", "l_own", "e_pf", "e_i1", "e_i2", "e_ia", "e_j", "e_self", "e_selb", "e_ox",
+               "e_oa", "e_ob", "e_off", "sent", "cp", "y0", "y1", "y2", "y3", "st"]
+              + [k + q for k in KINDS for q in ROLES]
+              + [k + q for k in ("gx", "qx", "oe", "ge", "qe") for q in ROLES + "O"]
+              + ["mm%d" % k for k in range(8)])
+
+CALLS = [
+    ([("e_selb", 1)], [("sel", "B", "straight", 0, 4), ("sel", "M", "straight", 4, 6), ("sel", "D", "straight", 6, 8)]),
+    ([("qxM", 1)], [("xc", "M", "mate", 0, 8)]),
+    ([("qxB", 1)], [("xc", "B", "die", 8, 16)]),
+    ([], [("xp", "M", "straight", 0, 4), ("xp", "B", "straight", 4, 8)]),
+    ([("qxD", 1)], [("xc", "D", "straight", 0, 8)]),
+    ([], [("xp", "D", "straight", 0, 8)]),
+    ([("qeB", 1)], [("ec", "B", "die", 8, 16)]),
+    ([], [("ep", "B", "die", 8, 16)]),
+    ([("qeM", 1)], [("ec", "M", "straight", 0, 8)]),
+    ([], [("ep", "M", "straight", 0, 8)]),
+    ([("qeD", 1)], [("ec", "D", "straight", 0, 8)]),
+    ([], [("ep", "D", "straight", 0, 8)]),
+]
 
 
 def u8(view):
@@ -65,202 +74,235 @@ def bits(engines):
     return sum(1 << e for e in engines)
 
 
-def helpers(r, T, topo):
-    c = T.cores[r]
-    l = 2 * (1 - r // 2)
-    other = [k for k in topo.cores_of(c) if topo.die(k) != topo.die(c)]
-    out = {}
-    for d in sorted((l, l + 1), key=lambda d: sum(topo.may_write(k, T.cores[d]) for k in other)):
-        k = [k for k in other if topo.may_write(k, T.cores[d]) and k not in out.values()][0]
-        out[d] = k
-    return out
+def roles(r, T, topo):
+    chip = [topo.chip(c) for c in T.cores]
+    mine = [d for d in range(N) if d == r or topo.same_plane(chip[d], chip[r])]
+    other = [d for d in range(N) if d not in mine]
+    i = mine.index(r)
+    return {"O": r, "B": mine[1 - i], "D": other[i], "M": other[1 - i]}
 
 
-def hand_on(g, core, T, topo, s, d):
-    dst = T.cores[d]
-    rid, pid, _ = topo.addr(dst)
-    n = len(topo.engines(core, dst))
-    a = (s % 2) * CAP
-    g.wait_ge(T.sem.hin, 8)
-    g.remote_dma(u8(T.xc2[:, a:a + CAP]), u8(T.hx[:]), T.sem.xq, T.sem.sent, pid, rid, topo.mask(core, dst))
-    g.wait_ge(T.sem.sent, n)
+def helper(s, role, way, T, topo):
+    c, dst = T.cores[s], T.cores[roles(s, T, topo)[role]]
+    if way == "mate":
+        ks = [k for k in range(NCORES) if topo.mates(topo.chip(k), topo.chip(dst)) and topo.die(k) == topo.die(c)
+              and topo.may_write(k, dst) and topo.may_write(c, k)]
+        return ks["MD".index(role)]
+    near = way == "near"
+    ks = [k for k in topo.cores_of(c) if k != c and (topo.die(k) == topo.die(c)) == near and topo.may_write(k, dst)]
+    if role == "B":
+        far = T.cores[roles(s, T, topo)["D"]]
+        return [k for k in ks if not topo.may_write(k, far)][0]
+    return ks["DM".index(role) % len(ks)]
+
+
+def landing(kind, s, T):
+    if kind == "sel":
+        return T.selin[:, s:s + 1]
+    w = CAP if kind[0] == "x" else F
+    view = T[kind][:, s * w:(s + 1) * w]
+    return u8(view) if kind[1] == "c" else view
+
+
+def leaving(kind, d, T):
+    if kind == "sel":
+        return T.selb[:, d:d + 1]
+    w = CAP if kind[0] == "x" else F
+    view = T["o" + kind][:, d * w:(d + 1) * w]
+    return u8(view) if kind[1] == "c" else view
+
+
+def arrives(kind, role, r, T, topo):
+    for _, items in CALLS:
+        for k, q, way, a, b in items:
+            if (k, q) == (kind, role):
+                s = roles(r, T, topo)[role]
+                n = b - a if way == "straight" else len(topo.engines(helper(s, role, way, T, topo), T.cores[r]))
+                return T.sem[kind + role], n
+
+
+def hand_on(g, core, T, topo):
+    sent = 0
+    for s in range(N):
+        for _, items in CALLS:
+            for kind, role, way, a, b in items:
+                if way != "straight" and helper(s, role, way, T, topo) == core:
+                    dst = T.cores[roles(s, T, topo)[role]]
+                    rid, pid, _ = topo.addr(dst)
+                    view = landing(kind, s, T)
+                    g.wait_ge(T.sem[kind + role], b - a)
+                    g.remote_dma(view, view, T.sem[kind + role], T.sem.sent, pid, rid, topo.mask(core, dst))
+                    sent += len(topo.engines(core, dst))
+    if sent:
+        g.wait_ge(T.sem.sent, sent)
 
 
 def rank_program(g, core, T, topo):
     r = T.rank_of(core)
     if r is None:
-        for s in range(N):
-            for d, k in helpers(s, T, topo).items():
-                if k == core:
-                    hand_on(g, core, T, topo, s, d)
+        hand_on(g, core, T, topo)
         return
     S, v, sc, te, sy = T.sem, g.vector, g.scalar, g.tensor, g.sync
     A, COPY = AluOpType, ActivationFunctionType.Copy
-    p, l = r ^ 1, 2 * (1 - r // 2)
-    h = l + 1
-    odd = r % 2
-    dst = {d: T.cores[d] for d in (p, l, h)}
-    help_ = helpers(r, T, topo)
-    sent = [0]
-
-    def one(out, in_, sem, d, mask, n):
-        rid, pid, _ = topo.addr(d)
-        g.remote_dma(out, in_, sem, S.sent, pid, rid, mask)
-        sent[0] += n
-
-    def two(items):
-        tr = []
-        for i, (out, in_, sem, d) in enumerate(items):
-            en = topo.engines(core, d)
-            half = en[:len(en) // 2] if i == 0 else en[len(en) // 2:]
-            rid, pid, _ = topo.addr(d)
-            tr.append(RemoteDMATransfer(dst_ids=[DstId(rid=rid, pnc=pid)], dma_engine_mask=bits(half), remote_sem=sem, src=in_, dst=out))
-            sent[0] += len(half)
-        g.remote_dma_fused(tr, local_sem=S.sent)
-
-    spp_e, spp_x = (CAP, 0) if odd else (0, 2 * F)
-    sq_e, sq_x = (CAP, 0) if odd else (0, F)
-    if odd:
-        sc1_e, sc1_x, own = 0, 2 * F, CAP
-    else:
-        sc1_e, sc1_x, own = PAIR, 0, 0
-    land_p = CAP if odd else 0
-    land_sp = CAP if odd else 0
-    land_sq = (CAP + F) if odd else 0
-    land_e = F if odd else 0
+    R = roles(r, T, topo)
 
     sc.dma_start(T.seli[0:1, 0:16], T.sel[:]).then_inc(S.l_sel, 16)
-    for k in range(4):
-        sc.dma_start(T.slist[16 * k:16 * k + 16, :], T.send[:]).then_inc(S.l_list, 16)
-    sc.dma_start(T.xs[:], T.x[:]).then_inc(S.l_x, 16)
+    sc.dma_start(T.slist[16:32, :], T.send[:]).then_inc(S.l_list, 16)
+    sy.dma_start(T.slist[0:16, :], T.send[:]).then_inc(S.l_list, 16)
+    sy.dma_start(T.po[0:16, 0:32], T.place[:]).then_inc(S.l_po, 16)
+    sy.dma_start(T.xs[:], T.x[:]).then_inc(S.l_x, 16)
     sy.dma_start(T.ws[:, 0:512], T.w[0:128, :]).then_inc(S.l_w, 16)
     sy.dma_start(T.ws[:, 512:1024], T.w[128:256, :]).then_inc(S.l_w, 16)
-    for k in range(4, 8):
-        sy.dma_start(T.slist[16 * k:16 * k + 16, :], T.send[:]).then_inc(S.l_list, 16)
-    sy.dma_start(T.po[:, 0:32], T.place[:]).then_inc(S.l_po, 16)
-    sy.dma_start(T.po[:, 32:64], T.of[:]).then_inc(S.l_po, 16)
+    sy.dma_start(T.po[16:32, 0:32], T.place[:]).then_inc(S.l_po, 16)
+    for k in range(2):
+        sy.dma_start(T.po[16 * k:16 * k + 16, 32:64], T.of[:]).then_inc(S.l_po, 16)
 
     g.iota(T.ip[:], [[0, 32]], 0, 1).then_inc(S.e_i1, 1)
     g.iota(T.ic[:], [[16, 32]], 0, 0).then_inc(S.e_i2, 1)
     g.wait_ge(S.e_self, 1)
     g.partition_broadcast(T.selb[:, 0:4], T.self_[0:1, 0:4], 128).then_inc(S.e_selb, 1)
-    g.wait_ge(S.e_selb, 1)
-    two([(T.selin[:, odd:odd + 1], T.selb[:, d:d + 1], S.selarr, dst[d]) for d in (l, h)])
-    m = topo.mask(core, dst[p])
-    n = len(topo.engines(core, dst[p]))
-    g.wait_ge(S.e_E, 1)
-    one(u8(T.epc[:]), u8(T.eco[:]), S.parr, dst[p], m, n)
-    g.wait_ge(S.e_xq, 2)
-    two([(u8(T.hx[:]), u8(T.xcq[:, i * CAP:(i + 1) * CAP]), S.hin, help_[d]) for i, d in enumerate((l, h))])
-    g.wait_ge(S.e_xp, 1)
-    one(u8(T.xc1[:, land_p:land_p + CAP]), u8(T.xcp[:]), S.parr, dst[p], m, n)
-    one(T.sc1[:, land_sp:land_sp + CAP + 2 * F], T.spp[:], S.parr, dst[p], m, n)
-    g.wait_ge(S.e_e, 2)
-    esem = S.eqh if odd else S.eql
-    two([(u8(T.eqc[:, land_e:land_e + F]), u8(T.ecq[:, i * F:(i + 1) * F]), esem, dst[d]) for i, d in enumerate((l, h))])
-    two([(T.sc2[:, land_sq:land_sq + CAP + F], q[:], esem, dst[d]) for q, d in ((T.sql, l), (T.sqh, h))])
-    g.wait_ge(S.sent, sent[0])
+    sent = 0
+    for waits, items in CALLS:
+        for name, val in waits:
+            g.wait_ge(S[name], val)
+        tr = []
+        for kind, role, way, a, b in items:
+            dst = T.cores[R[role]] if way == "straight" else helper(r, role, way, T, topo)
+            rid, pid, _ = topo.addr(dst)
+            tr.append(RemoteDMATransfer(dst_ids=[DstId(rid=rid, pnc=pid)], dma_engine_mask=bits(topo.engines(core, dst)[a:b]),
+                                        remote_sem=S[kind + role], src=leaving(kind, R[role], T), dst=landing(kind, r, T)))
+            sent += b - a
+        g.remote_dma_fused(tr, local_sem=S.sent)
+        if OWN_BY_DMA and items[0][0] == "sel":
+            g.wait_ge(S.oeO, 1)
+            g.indirect_dma_start(T.et[:, 512 * r:512 * (r + 1)], None, T.w[:], IndirectOffsetOnAxis(ap=T.row[:, 0:1], axis=0),
+                                 bounds_check=2 * F - 1).then_inc(S.l_own, 16)
+    g.wait_ge(S.sent, sent)
+
+    def pick(q, out, window, offsets, sem):
+        if q is v:
+            v.tensor_copy(out, window.indirect(offsets)).then_inc(sem, 1)
+        else:
+            sc.activation(out, window.indirect(offsets), COPY).then_inc(sem, 1)
+
+    def columns(q, role, ts):
+        d = R[role]
+        for t in ts:
+            pick(q, T.xt[:, 4 * d * CAP + t:4 * (d + 1) * CAP:4], T.xs[:, t:4 * COLS],
+                 T.ox[:, d * CAP // 16:(d + 1) * CAP // 16], S["gx" + role])
+
+    def pack_columns(role):
+        d = R[role]
+        c, p = (T.xc, T.xp) if role == "O" else (T.oxc, T.oxp)
+        v.wait_ge(S["gx" + role], 4)
+        v.quantize_mx(c[:, d * CAP:(d + 1) * CAP], p[:, d * CAP:(d + 1) * CAP],
+                      T.xt[:, 4 * d * CAP:4 * (d + 1) * CAP]).then_inc(S["qx" + role], 1)
+
+    def ask(role):
+        d = R[role]
+        if role == "O":
+            v.wait_ge(S.e_selb, 1)
+            col = T.selb[:, d:d + 1]
+        else:
+            v.wait_ge(*arrives("sel", role, r, T, topo))
+            col = T.selin[:, d:d + 1]
+        v.tensor_scalar(T.oe[:, 32 * d:32 * d + 32], T.jj[:], col, None, A.add).then_inc(S["oe" + role], 1)
+
+    def expert(q, role, a, b):
+        d = R[role]
+        q.wait_ge(S["oe" + role], 1)
+        pick(q, T.et[:, 512 * d + a:512 * d + b], T.ws[:], T.oe[:, 32 * d + a // 16:32 * d + b // 16], S["ge" + role])
+
+    def pack_expert(role):
+        d = R[role]
+        c, p = (T.ec, T.ep) if role == "O" else (T.oec, T.oep)
+        v.wait_ge(*((S.l_own, 16) if role == "O" and OWN_BY_DMA else (S["ge" + role], 2)))
+        v.quantize_mx(c[:, d * F:(d + 1) * F], p[:, d * F:(d + 1) * F], T.et[:, 512 * d:512 * (d + 1)]).then_inc(S["qe" + role], 1)
 
     v.wait_ge(S.e_i1, 1)
     v.tensor_scalar(T.ia[:], T.ip[:], 15, None, A.bitwise_and).then_inc(S.e_ia, 1)
+    v.tensor_copy(T.pf[:, 0:1], T.ip[:, 0:1]).then_inc(S.e_pf, 1)
     v.wait_ge(S.e_i2, 1)
     v.wait_ge(S.e_ia, 1)
     v.tensor_tensor(T.jj[:], T.ia[:], T.ic[:], A.add).then_inc(S.e_j, 1)
     v.wait_ge(S.l_sel, 16)
     v.tensor_scalar(T.self_[0:1, :], T.seli[0:1, :], 512.0, 0.0, A.mult, A.max).then_inc(S.e_self, 1)
-    v.wait_ge(S.l_list, 128)
-    v.tensor_scalar(T.ox[:], T.slist[:], 4.0, 0.0, A.mult, A.max).then_inc(S.e_ox, 1)
-    v.wait_ge(S.l_w, 32)
-    v.quantize_mx(T.eco[:], T.spp[:, spp_e:spp_e + 2 * F], T.ws[:]).then_inc(S.e_E, 1)
-
-    def gather(tile, n, first, sem):
-        o = T.ox[:, first // 16:(first + n) // 16]
-        for t in range(2):
-            v.tensor_copy(tile[:, t:4 * n:4], T.xs[:, t:4 * COLS].indirect(o)).then_inc(sem, 1)
-        for t in range(2, 4):
-            sc.activation(tile[:, t:4 * n:4], T.xs[:, t:4 * COLS].indirect(o), COPY).then_inc(sem, 1)
-        v.wait_ge(sem, 4)
-
-    for q in (v, sc):
-        q.wait_ge(S.l_x, 16)
-        q.wait_ge(S.e_ox, 1)
-    gather(T.xtq, PAIR, l * CAP, S.e_gq)
-    for i, q in enumerate((T.sql, T.sqh)):
-        v.quantize_mx(T.xcq[:, i * CAP:(i + 1) * CAP], q[:, sq_x:sq_x + CAP], T.xtq[:, 4 * i * CAP:4 * (i + 1) * CAP]).then_inc(S.e_xq, 1)
-    gather(T.xtp, CAP, p * CAP, S.e_gp)
-    v.quantize_mx(T.xcp[:], T.spp[:, spp_x:spp_x + CAP], T.xtp[:]).then_inc(S.e_xp, 1)
-    v.wait_ge(S.selarr, 8)
+    v.wait_ge(S.l_list, 32)
+    for k in range(4):
+        v.tensor_scalar(T.ox[32 * k:32 * k + 32, :], T.slist[:], 4.0, 0.0, A.mult, A.max).then_inc(S.e_ox, 1)
     v.wait_ge(S.e_j, 1)
-    for i in range(2):
-        v.tensor_scalar(T.oe[:, 32 * i:32 * i + 32], T.jj[:], T.selin[:, i:i + 1], None, A.add).then_inc(S.e_oe, 1)
+    v.wait_ge(S.e_pf, 1)
+    if OWN_BY_DMA:
+        v.wait_ge(S.e_selb, 1)
+        v.tensor_scalar(T.row[:, 0:1], T.selb[:, r:r + 1], F / 512.0, T.pf[:, 0:1], A.mult, A.add).then_inc(S.oeO, 1)
+    else:
+        ask("O")
     for q in (v, sc):
-        q.wait_ge(S.e_oe, 2)
-    sc.wait_ge(S.l_w, 32)
-    v.tensor_copy(T.et[:, 0:512], T.ws[:, 0:1024].indirect(T.oe[:, 0:32])).then_inc(S.e_ge, 1)
-    sc.activation(T.et[:, 512:1024], T.ws[:, 0:1024].indirect(T.oe[:, 32:64]), COPY).then_inc(S.e_ge, 1)
-    v.wait_ge(S.e_ge, 2)
-    for i, q in enumerate((T.sql, T.sqh)):
-        v.quantize_mx(T.ecq[:, i * F:(i + 1) * F], q[:, sq_e:sq_e + F], T.et[:, 512 * i:512 * (i + 1)]).then_inc(S.e_e, 1)
-    gather(T.xto, CAP, r * CAP, S.e_go)
-    so = sc1_x + own
-    v.quantize_mx(T.xc1[:, own:own + CAP], T.sc1[:, so:so + CAP], T.xto[:]).then_inc(S.e_xo, 1)
-    v.wait_ge(S.l_po, 32)
-    v.wait_ge(S.e_selb, 1)
-    v.tensor_scalar(T.base[:, 0:1], T.selb[0:16, r:r + 1], ALL / 512.0, None, A.mult).then_inc(S.e_base, 1)
-    v.tensor_scalar(T.base[:, 1:2], T.selb[0:16, p:p + 1], ALL / 512.0, 2.0 * ALL, A.mult, A.add).then_inc(S.e_base, 1)
-    v.wait_ge(S.e_base, 2)
-    of, place = T.po[:, 32:64], T.po[:, 0:32]
-    for i, (who, b) in enumerate(((r, T.base[:, 0:1]), (p, T.base[:, 1:2]), (l, 4.0 * ALL), (h, 5.0 * ALL))):
-        v.tensor_scalar(T.oa[:, 32 * i:32 * i + 32], of, float(who), b, A.is_equal, A.mult).then_inc(S.e_m, 1)
-    v.wait_ge(S.e_m, 4)
-    v.tensor_tensor(T.ob[:, 0:64], T.oa[:, 0:64], T.oa[:, 64:128], A.add).then_inc(S.e_s1, 1)
-    v.wait_ge(S.e_s1, 1)
-    v.tensor_tensor(T.ob[:, 64:96], T.ob[:, 0:32], T.ob[:, 32:64], A.add).then_inc(S.e_s2, 1)
-    v.wait_ge(S.e_s2, 1)
-    v.tensor_tensor(T.ob[:, 96:128], T.ob[:, 64:96], place, A.add).then_inc(S.e_s3, 1)
-    v.wait_ge(S.e_s3, 1)
-    v.tensor_copy(T.off1[:], T.ob[:, 96:128]).then_inc(S.e_off, 1)
-    sy.wait_ge(S.e_off, 1)
-    for k in range(8):
-        sy.dma_start(T.off[16 * k:16 * k + 16, :], T.off1[:]).then_inc(S.l_off, 16)
+        q.wait_ge(S.e_ox, 4)
+        q.wait_ge(S.l_x, 16)
+    CUT = 192
+    for role in "MB":
+        columns(v, role, (0, 1))
+        columns(sc, role, (2, 3))
+        pack_columns(role)
+    columns(sc, "D", (1, 2, 3))
+    columns(v, "D", (0,))
+    for role in "BMD":
+        ask(role)
+    pack_columns("D")
+    for q in (v, sc):
+        q.wait_ge(S.l_w, 32)
+    for role in "BMD":
+        expert(v, role, 0, CUT)
+        expert(sc, role, CUT, 512)
+        pack_expert(role)
+    v.wait_ge(S.l_po, 64)
+    v.tensor_scalar(T.oa[:], T.po[:, 32:64], float(ALL), None, A.mult).then_inc(S.e_oa, 1)
+    if not OWN_BY_DMA:
+        expert(v, "O", 0, CUT)
+        expert(sc, "O", CUT, 512)
+    v.wait_ge(S.e_oa, 1)
+    v.tensor_tensor(T.ob[:], T.oa[:], T.po[:, 0:32], A.add).then_inc(S.e_ob, 1)
+    pack_expert("O")
+    columns(sc, "O", (1, 2, 3))
+    columns(v, "O", (0,))
+    v.wait_ge(S.e_ob, 1)
+    for k in range(4):
+        v.tensor_copy(T.off[32 * k:32 * k + 32, :], T.ob[:]).then_inc(S.e_off, 1)
+    pack_columns("O")
 
-    def expert(e):
-        a = (e % 2) * F
-        if e < 2:
-            return T.eco[:, a:a + F], T.spp[:, spp_e + a:spp_e + a + F]
-        if e < 4:
-            return T.epc[:, a:a + F], T.sc1[:, sc1_e + a:sc1_e + a + F]
-        b = 0 if e == 4 else F + PAIR
-        return T.eqc[:, a:a + F], T.sc2[:, b:b + F]
-    group = {0: (T.xc1[:], T.sc1[:, sc1_x:sc1_x + PAIR], r // 2), 1: (T.xc2[:], T.sc2[:, F:F + PAIR], 1 - r // 2)}
-    own_w, p_w, l_w, h_w, x_w = (S.e_E, 1), (S.parr, 3 * n), (S.eql, 8), (S.eqh, 8), (S.xq, 16)
-    order = [(0, 0, [own_w, p_w, (S.e_xo, 1)]), (1, 0, []), (2, 0, []), (3, 0, []),
-             (4, 0, [l_w]), (5, 0, [h_w]), (4, 1, [x_w]), (5, 1, []), (0, 1, []), (1, 1, []), (2, 1, []), (3, 1, [])]
-    for k, (e, gr, waits) in enumerate(order):
-        for sem, val in waits:
-            te.wait_ge(sem, val)
-        if k >= 8:
-            te.wait_ge(S["cp%d" % (k - 8)], 1)
-        bank = 512 * (k % 8)
-        W, Ws = expert(e)
-        X, Xs, pos = group[gr]
-        te.matmul_mx(T.ps[:, bank:bank + PAIR], W, Ws, X, Xs, True, True).then_inc(S["mm%d" % k], 1)
-        q = sc if k % 2 else v
+    def have(kind, role):
+        if role == "O":
+            return [(S["q" + kind + "O"], 1)]
+        return [arrives(kind + "c", role, r, T, topo), arrives(kind + "p", role, r, T, topo)]
+    mine, far = r // 2, 1 - r // 2
+    by_rank = {d: q for q, d in R.items()}
+    order = [("O", far), ("O", mine), ("M", far), ("M", mine), ("D", far), ("D", mine), ("B", far), ("B", mine)]
+    seen = []
+    for k, (role, pair) in enumerate(order):
+        for need in [("e", role), ("x", by_rank[2 * pair]), ("x", by_rank[2 * pair + 1])]:
+            if need not in seen:
+                seen.append(need)
+                for sem, val in have(*need):
+                    te.wait_ge(sem, val)
+        e, a = R[role], pair * PAIR
+        bank = T.ps[:, 512 * k:512 * k + PAIR]
+        te.matmul_mx(bank, T.ec[:, e * F:(e + 1) * F], T.ep[:, e * F:(e + 1) * F],
+                     T.xc[:, a:a + PAIR], T.xp[:, a:a + PAIR], True, True).then_inc(S["mm%d" % k], 1)
+        q = sc if k % 2 == 0 else v
         q.wait_ge(S["mm%d" % k], 1)
-        o = T.res[:, e * ALL + pos * PAIR:e * ALL + (pos + 1) * PAIR]
-        if k % 2:
-            sc.activation(o, T.ps[:, bank:bank + PAIR], COPY).then_inc(S["cp%d" % k], 1)
+        o = T.res[:, e * ALL + a:e * ALL + a + PAIR]
+        if q is sc:
+            sc.activation(o, bank, COPY).then_inc(S.cp, 1)
         else:
-            v.tensor_copy(o, T.ps[:, bank:bank + PAIR]).then_inc(S["cp%d" % k], 1)
+            v.tensor_copy(o, bank).then_inc(S.cp, 1)
 
     for q in (v, sc):
-        q.wait_ge(S.l_off, 128)
-        for k in range(12):
-            q.wait_ge(S["cp%d" % k], 1)
-    v.tensor_copy(T.yb[:, 0:256], T.res[:].indirect(T.off[:, 0:16])).then_inc(S.e_yv, 1)
-    sc.activation(T.yb[:, 256:512], T.res[:].indirect(T.off[:, 16:32]), COPY).then_inc(S.e_ys, 1)
-    sy.wait_ge(S.e_yv, 1)
-    sy.dma_start(T.y[:, 0:256], T.yb[:, 0:256]).then_inc(S.st, 16)
-    sc.wait_ge(S.e_ys, 1)
-    sc.dma_start(T.y[:, 256:512], T.yb[:, 256:512]).then_inc(S.st, 16)
+        q.wait_ge(S.e_off, 4)
+        q.wait_ge(S.cp, len(order))
+    for k, q in enumerate((v, sc)):
+        pick(q, T.yb[:, 256 * k:256 * k + 256], T.res[:], T.off[:, 16 * k:16 * k + 16], S["y%d" % k])
+    for k, q in enumerate((sy, sc)):
+        q.wait_ge(S["y%d" % k], 1)
+        q.dma_start(T.y[:, 256 * k:256 * k + 256], T.yb[:, 256 * k:256 * k + 256]).then_inc(S.st, 16)
     sy.wait_ge(S.st, 32)

@@ -1,4 +1,4 @@
-from concourse.bass import DstId, RemoteDMATransfer, IndirectOffsetOnAxis
+from concourse.bass import DstId, RemoteDMATransfer
 from concourse.mybir import dt, AluOpType, ActivationFunctionType
 
 N, COLS, CAP, F = 4, 512, 192, 128
@@ -7,27 +7,28 @@ PAIR = 2 * CAP
 ALL = N * CAP
 CODES = "float8_e4m3fn_x4"
 ROLES = "MBD"
-OWN_BY_DMA = False
+BOTH = ""
+EXPERTS = N + len(BOTH)
+XCUTS = ((0, 16), (16, 48), (48, 80), (80, 128))
 
 SCRATCH = {
     "xs": ("sbuf", [128, 4 * COLS], "bfloat16"),
     "ws": ("sbuf", [128, 8 * F], "bfloat16"),
     "slist": ("sbuf", [32, ALL // 16], "int32"),
     "seli": ("sbuf", [128, 16], "int32"),
-    "po": ("sbuf", [32, 64], "int32"),
+    "po": ("sbuf", [64, 64], "int32"),
     "ip": ("sbuf", [128, 32], "int32"),
     "ia": ("sbuf", [128, 32], "int32"),
     "ic": ("sbuf", [128, 32], "int32"),
     "jj": ("sbuf", [128, 32], "float32"),
-    "pf": ("sbuf", [128, 4], "float32"),
-    "row": ("sbuf", [128, 4], "int32"),
+    "junk": ("sbuf", [128, 512], "float32"),
     "self_": ("sbuf", [128, 16], "float32"),
     "selb": ("sbuf", [128, 4], "float32"),
     "selin": ("sbuf", [128, 4], "float32"),
     "ox": ("sbuf", [128, ALL // 16], "uint16"),
     "oe": ("sbuf", [128, 32 * N], "uint16"),
-    "oa": ("sbuf", [32, 32], "float32"),
-    "ob": ("sbuf", [32, 32], "float32"),
+    "edge": ("sbuf", [64, 4], "float32"),
+    "oa": ("sbuf", [64, 32 * 12], "float32"),
     "off": ("sbuf", [128, 32], "uint16"),
     "xt": ("sbuf", [128, 4 * ALL], "bfloat16"),
     "et": ("sbuf", [128, 4 * F * N], "bfloat16"),
@@ -35,35 +36,47 @@ SCRATCH = {
     "oxp": ("sbuf", [128, ALL], "uint8"),
     "oec": ("sbuf", [128, N * F], CODES),
     "oep": ("sbuf", [128, N * F], "uint8"),
+    "bec": ("sbuf", [128, 2 * F], CODES),
+    "bep": ("sbuf", [128, 2 * F], "uint8"),
     "xc": ("sbuf", [128, ALL], CODES),
     "xp": ("sbuf", [128, ALL], "uint8"),
-    "ec": ("sbuf", [128, N * F], CODES),
-    "ep": ("sbuf", [128, N * F], "uint8"),
+    "ec": ("sbuf", [128, EXPERTS * F], CODES),
+    "ep": ("sbuf", [128, EXPERTS * F], "uint8"),
     "ps": ("psum", [128, 4096], "float32"),
-    "res": ("sbuf", [128, N * ALL], "float32"),
+    "res": ("sbuf", [128, EXPERTS * ALL], "float32"),
     "yb": ("sbuf", [128, COLS], "float32"),
 }
-KINDS = ("sel", "xc", "xp", "ec", "ep")
-SEMAPHORES = (["l_sel", "l_list", "l_w", "l_x", "l_po", "l_own", "e_pf", "e_i1", "e_i2", "e_ia", "e_j", "e_self", "e_selb", "e_ox",
-               "e_oa", "e_ob", "e_off", "sent", "cp", "y0", "y1", "y2", "y3", "st"]
-              + [k + q for k in KINDS for q in ROLES]
-              + [k + q for k in ("gx", "qx", "oe", "ge", "qe") for q in ROLES + "O"]
-              + ["mm%d" % k for k in range(8)])
 
 CALLS = [
-    ([("e_selb", 1)], [("sel", "B", "straight", 0, 4), ("sel", "M", "straight", 4, 6), ("sel", "D", "straight", 6, 8)]),
-    ([("qxM", 1)], [("xc", "M", "mate", 0, 8)]),
-    ([("qxB", 1)], [("xc", "B", "die", 8, 16)]),
-    ([], [("xp", "M", "straight", 0, 4), ("xp", "B", "straight", 4, 8)]),
-    ([("qxD", 1)], [("xc", "D", "straight", 0, 8)]),
+    (["e_selb"], [("sel", "B", "straight", 0, 8)]),
+    ([], [("sel", "M", "straight", 0, 8)]),
+    ([], [("sel", "D", "straight", 0, 8)]),
+    (["qxM"], [("xp", "M", "mate", 0, 8), ("xp", "B", "die", 8, 16)]),
+    ([], [("xc", "M", "mate", 0, 8), ("xc", "B", "die", 8, 16)]),
+    (["qxD"], [("xc", "D", "straight", 0, 8)]),
     ([], [("xp", "D", "straight", 0, 8)]),
-    ([("qeB", 1)], [("ec", "B", "die", 8, 16)]),
-    ([], [("ep", "B", "die", 8, 16)]),
-    ([("qeM", 1)], [("ec", "M", "straight", 0, 8)]),
-    ([], [("ep", "M", "straight", 0, 8)]),
-    ([("qeD", 1)], [("ec", "D", "straight", 0, 8)]),
+    (["qeB"], [("ec", "B", "die", 8, 16)]),
+    (["qeM"], [("ec", "M", "straight", 0, 8)]),
+    ([], [("ep", "M", "straight", 0, 4), ("ep", "B", "straight", 4, 8)]),
+    (["qeD"], [("ec", "D", "straight", 0, 8)]),
     ([], [("ep", "D", "straight", 0, 8)]),
 ]
+STEPS = [("columns", "MB", 768), ("pack_columns", "MB"),
+         ("columns", "D", 192), ("ask", "B"), ("pack_columns", "D"), ("ask", "M"),
+         ("expert", "B", 192), ("ask", "D"), ("pack_expert", "B"), ("expert", "M", 192), ("pack_expert", "M"),
+         ("expert", "D", 192), ("pack_expert", "D"), ("expert", "O", 0), ("places", 0),
+         ("columns", "O", 384), ("places", 1), ("pack_expert", "O"), ("places", 2), ("pack_columns", "O")]
+COPIERS = "svsvsvsvsv"
+ORDER = [("O", 0, "OD"), ("O", 0, "MB"), ("M", 0, "OD"), ("M", 0, "MB"), ("B", 0, "OD"), ("B", 0, "MB"),
+         ("D", 0, "M"), ("D", 0, "B"), ("D", 0, "O"), ("D", 0, "D")]
+BANKS = 8
+
+SEMAPHORES = (["l_sel", "l_list", "l_w", "l_x", "l_po", "e_i1", "e_i2", "e_ia", "e_j", "e_self", "e_selb", "e_ox",
+               "e_edge", "e_off", "both", "sent", "cp", "y0", "y1", "y2", "y3", "st"]
+              + [k + q for k in ("sel", "xc", "xp", "ec", "ep") for q in ROLES]
+              + [k + q for k in ("gx", "qx", "oe", "ge", "qe") for q in ROLES + "O"]
+              + ["oa%d" % k for k in range(6)] + ["mm%d" % k for k in range(len(ORDER))]
+              + ["cp%d" % k for k in range(len(ORDER) - BANKS)])
 
 
 def u8(view):
@@ -87,7 +100,7 @@ def helper(s, role, way, T, topo):
     if way == "mate":
         ks = [k for k in range(NCORES) if topo.mates(topo.chip(k), topo.chip(dst)) and topo.die(k) == topo.die(c)
               and topo.may_write(k, dst) and topo.may_write(c, k)]
-        return ks["MD".index(role)]
+        return ks[0]
     near = way == "near"
     ks = [k for k in topo.cores_of(c) if k != c and (topo.die(k) == topo.die(c)) == near and topo.may_write(k, dst)]
     if role == "B":
@@ -96,19 +109,31 @@ def helper(s, role, way, T, topo):
     return ks["DM".index(role) % len(ks)]
 
 
-def landing(kind, s, T):
+def place_of(h, r, T, topo):
+    R = roles(r, T, topo)
+    return h + sum(R[q] < h for q in BOTH)
+
+
+def landing(kind, s, role, T, topo):
     if kind == "sel":
         return T.selin[:, s:s + 1]
-    w = CAP if kind[0] == "x" else F
-    view = T[kind][:, s * w:(s + 1) * w]
+    if kind[0] == "x":
+        view = T[kind][:, s * CAP:(s + 1) * CAP]
+    else:
+        e = place_of(s, roles(s, T, topo)[role], T, topo)
+        view = T[kind][:, e * F:(e + 1 + (role in BOTH)) * F]
     return u8(view) if kind[1] == "c" else view
 
 
-def leaving(kind, d, T):
+def leaving(kind, s, role, T, topo):
+    d = roles(s, T, topo)[role]
     if kind == "sel":
         return T.selb[:, d:d + 1]
-    w = CAP if kind[0] == "x" else F
-    view = T["o" + kind][:, d * w:(d + 1) * w]
+    if kind[0] == "e" and role in BOTH:
+        view = T["b" + kind][:]
+    else:
+        w = CAP if kind[0] == "x" else F
+        view = T["o" + kind][:, d * w:(d + 1) * w]
     return u8(view) if kind[1] == "c" else view
 
 
@@ -123,13 +148,13 @@ def arrives(kind, role, r, T, topo):
 
 def hand_on(g, core, T, topo):
     sent = 0
-    for s in range(N):
-        for _, items in CALLS:
-            for kind, role, way, a, b in items:
+    for _, items in CALLS:
+        for kind, role, way, a, b in items:
+            for s in range(N):
                 if way != "straight" and helper(s, role, way, T, topo) == core:
                     dst = T.cores[roles(s, T, topo)[role]]
                     rid, pid, _ = topo.addr(dst)
-                    view = landing(kind, s, T)
+                    view = landing(kind, s, role, T, topo)
                     g.wait_ge(T.sem[kind + role], b - a)
                     g.remote_dma(view, view, T.sem[kind + role], T.sem.sent, pid, rid, topo.mask(core, dst))
                     sent += len(topo.engines(core, dst))
@@ -148,13 +173,13 @@ def rank_program(g, core, T, topo):
 
     sc.dma_start(T.seli[0:1, 0:16], T.sel[:]).then_inc(S.l_sel, 16)
     sc.dma_start(T.slist[16:32, :], T.send[:]).then_inc(S.l_list, 16)
-    sy.dma_start(T.slist[0:16, :], T.send[:]).then_inc(S.l_list, 16)
-    sy.dma_start(T.po[0:16, 0:32], T.place[:]).then_inc(S.l_po, 16)
-    sy.dma_start(T.xs[:], T.x[:]).then_inc(S.l_x, 16)
+    sc.dma_start(T.slist[0:16, :], T.send[:]).then_inc(S.l_list, 16)
+    for a, b in XCUTS:
+        sy.dma_start(T.xs[a:b, :], T.x[a:b, :]).then_inc(S.l_x, 16)
     sy.dma_start(T.ws[:, 0:512], T.w[0:128, :]).then_inc(S.l_w, 16)
     sy.dma_start(T.ws[:, 512:1024], T.w[128:256, :]).then_inc(S.l_w, 16)
-    sy.dma_start(T.po[16:32, 0:32], T.place[:]).then_inc(S.l_po, 16)
-    for k in range(2):
+    for k in range(4):
+        sy.dma_start(T.po[16 * k:16 * k + 16, 0:32], T.place[:]).then_inc(S.l_po, 16)
         sy.dma_start(T.po[16 * k:16 * k + 16, 32:64], T.of[:]).then_inc(S.l_po, 16)
 
     g.iota(T.ip[:], [[0, 32]], 0, 1).then_inc(S.e_i1, 1)
@@ -163,20 +188,17 @@ def rank_program(g, core, T, topo):
     g.partition_broadcast(T.selb[:, 0:4], T.self_[0:1, 0:4], 128).then_inc(S.e_selb, 1)
     sent = 0
     for waits, items in CALLS:
-        for name, val in waits:
-            g.wait_ge(S[name], val)
+        for name in waits:
+            g.wait_ge(S[name], 1)
         tr = []
         for kind, role, way, a, b in items:
             dst = T.cores[R[role]] if way == "straight" else helper(r, role, way, T, topo)
             rid, pid, _ = topo.addr(dst)
             tr.append(RemoteDMATransfer(dst_ids=[DstId(rid=rid, pnc=pid)], dma_engine_mask=bits(topo.engines(core, dst)[a:b]),
-                                        remote_sem=S[kind + role], src=leaving(kind, R[role], T), dst=landing(kind, r, T)))
+                                        remote_sem=S[kind + role], src=leaving(kind, r, role, T, topo),
+                                        dst=landing(kind, r, role, T, topo)))
             sent += b - a
         g.remote_dma_fused(tr, local_sem=S.sent)
-        if OWN_BY_DMA and items[0][0] == "sel":
-            g.wait_ge(S.oeO, 1)
-            g.indirect_dma_start(T.et[:, 512 * r:512 * (r + 1)], None, T.w[:], IndirectOffsetOnAxis(ap=T.row[:, 0:1], axis=0),
-                                 bounds_check=2 * F - 1).then_inc(S.l_own, 16)
     g.wait_ge(S.sent, sent)
 
     def pick(q, out, window, offsets, sem):
@@ -185,18 +207,34 @@ def rank_program(g, core, T, topo):
         else:
             sc.activation(out, window.indirect(offsets), COPY).then_inc(sem, 1)
 
-    def columns(q, role, ts):
-        d = R[role]
-        for t in ts:
-            pick(q, T.xt[:, 4 * d * CAP + t:4 * (d + 1) * CAP:4], T.xs[:, t:4 * COLS],
-                 T.ox[:, d * CAP // 16:(d + 1) * CAP // 16], S["gx" + role])
+    def slots(who):
+        ds = sorted(R[q] for q in who)
+        assert ds[-1] - ds[0] == len(ds) - 1
+        return ds[0] * CAP, (ds[-1] + 1) * CAP
 
-    def pack_columns(role):
-        d = R[role]
-        c, p = (T.xc, T.xp) if role == "O" else (T.oxc, T.oxp)
-        v.wait_ge(S["gx" + role], 4)
-        v.quantize_mx(c[:, d * CAP:(d + 1) * CAP], p[:, d * CAP:(d + 1) * CAP],
-                      T.xt[:, 4 * d * CAP:4 * (d + 1) * CAP]).then_inc(S["qx" + role], 1)
+    calls = {}
+    have_w = []
+
+    def need_w(q):
+        if q not in have_w:
+            have_w.append(q)
+            (v if q == "v" else sc).wait_ge(S.l_w, 32)
+
+    def columns(who, share):
+        a, b = slots(who)
+        calls["x" + who] = 0
+        for t in range(4):
+            cut = a + min(b - a, max(0, share - t * (b - a)))
+            for q, lo, hi in ((v, a, cut), (sc, cut, b)):
+                if hi > lo:
+                    pick(q, T.xt[:, 4 * lo + t:4 * hi:4], T.xs[:, t:4 * COLS], T.ox[:, lo // 16:hi // 16], S["gx" + who[0]])
+                    calls["x" + who] += 1
+
+    def pack_columns(who):
+        a, b = slots(who)
+        c, p = (T.xc, T.xp) if who == "O" else (T.oxc, T.oxp)
+        v.wait_ge(S["gx" + who[0]], calls["x" + who])
+        v.quantize_mx(c[:, a:b], p[:, a:b], T.xt[:, 4 * a:4 * b]).then_inc(S["qx" + who[0]], 1)
 
     def ask(role):
         d = R[role]
@@ -208,20 +246,50 @@ def rank_program(g, core, T, topo):
             col = T.selin[:, d:d + 1]
         v.tensor_scalar(T.oe[:, 32 * d:32 * d + 32], T.jj[:], col, None, A.add).then_inc(S["oe" + role], 1)
 
-    def expert(q, role, a, b):
+    def expert(role, share, now="vs"):
         d = R[role]
-        q.wait_ge(S["oe" + role], 1)
-        pick(q, T.et[:, 512 * d + a:512 * d + b], T.ws[:], T.oe[:, 32 * d + a // 16:32 * d + b // 16], S["ge" + role])
+        calls.setdefault("e" + role, 0)
+        for name, q, a, b in (("v", v, 0, share), ("s", sc, share, 4 * F)):
+            if b > a and name in now:
+                need_w(name)
+                q.wait_ge(S["oe" + role], 1)
+                pick(q, T.et[:, 512 * d + a:512 * d + b], T.ws[:], T.oe[:, 32 * d + a // 16:32 * d + b // 16], S["ge" + role])
+                calls["e" + role] += 1
 
     def pack_expert(role):
         d = R[role]
-        c, p = (T.ec, T.ep) if role == "O" else (T.oec, T.oep)
-        v.wait_ge(*((S.l_own, 16) if role == "O" and OWN_BY_DMA else (S["ge" + role], 2)))
-        v.quantize_mx(c[:, d * F:(d + 1) * F], p[:, d * F:(d + 1) * F], T.et[:, 512 * d:512 * (d + 1)]).then_inc(S["qe" + role], 1)
+        e, c, p = (place_of(d, r, T, topo), T.ec, T.ep) if role == "O" else (d, T.oec, T.oep)
+        v.wait_ge(S["ge" + role], calls["e" + role])
+        v.quantize_mx(c[:, e * F:(e + 1) * F], p[:, e * F:(e + 1) * F], T.et[:, 512 * d:512 * (d + 1)]).then_inc(S["qe" + role], 1)
+
+    def pack_both():
+        need_w("v")
+        v.quantize_mx(T.bec[:], T.bep[:], T.ws[:]).then_inc(S.both, 1)
+
+    def places(step):
+        part = [T.oa[:, 32 * k:32 * k + 32] for k in range(12)]
+        n = len(BOTH)
+        if step == 0:
+            v.wait_ge(S.l_po, 128)
+            v.tensor_scalar(part[0], T.po[:, 32:64], float(ALL), None, A.mult).then_inc(S.oa0, 1)
+            if n:
+                v.wait_ge(S.e_edge, n)
+            for k in range(n):
+                v.tensor_scalar(part[1 + k], T.po[:, 32:64], T.edge[:, k:k + 1], float(ALL), A.is_ge, A.mult).then_inc(S.oa0, 1)
+            return
+        if step == 1:
+            v.wait_ge(S.oa0, 1 + n)
+            v.tensor_tensor(part[6], part[0], T.po[:, 0:32], A.add).then_inc(S.oa1, 1)
+            return
+        for k in range(n):
+            v.wait_ge(S["oa%d" % (1 + k)], 1)
+            v.tensor_tensor(part[7 + k], part[6 + k], part[1 + k], A.add).then_inc(S["oa%d" % (2 + k)], 1)
+        v.wait_ge(S["oa%d" % (1 + n)], 1)
+        for k in range(2):
+            v.tensor_copy(T.off[64 * k:64 * k + 64, :], part[6 + n]).then_inc(S.e_off, 1)
 
     v.wait_ge(S.e_i1, 1)
     v.tensor_scalar(T.ia[:], T.ip[:], 15, None, A.bitwise_and).then_inc(S.e_ia, 1)
-    v.tensor_copy(T.pf[:, 0:1], T.ip[:, 0:1]).then_inc(S.e_pf, 1)
     v.wait_ge(S.e_i2, 1)
     v.wait_ge(S.e_ia, 1)
     v.tensor_tensor(T.jj[:], T.ia[:], T.ic[:], A.add).then_inc(S.e_j, 1)
@@ -231,78 +299,56 @@ def rank_program(g, core, T, topo):
     for k in range(4):
         v.tensor_scalar(T.ox[32 * k:32 * k + 32, :], T.slist[:], 4.0, 0.0, A.mult, A.max).then_inc(S.e_ox, 1)
     v.wait_ge(S.e_j, 1)
-    v.wait_ge(S.e_pf, 1)
-    if OWN_BY_DMA:
-        v.wait_ge(S.e_selb, 1)
-        v.tensor_scalar(T.row[:, 0:1], T.selb[:, r:r + 1], F / 512.0, T.pf[:, 0:1], A.mult, A.add).then_inc(S.oeO, 1)
-    else:
+    v.wait_ge(S.e_selb, 1)
+    if "O" not in BOTH:
         ask("O")
+    for k, role in enumerate(BOTH):
+        d = R[role]
+        v.tensor_scalar(T.edge[:, k:k + 1], T.selb[0:64, d:d + 1], -1 / 512.0, d + 1.0, A.mult, A.add).then_inc(S.e_edge, 1)
     for q in (v, sc):
         q.wait_ge(S.e_ox, 4)
-        q.wait_ge(S.l_x, 16)
-    CUT = 192
-    for role in "MB":
-        columns(v, role, (0, 1))
-        columns(sc, role, (2, 3))
-        pack_columns(role)
-    columns(sc, "D", (1, 2, 3))
-    columns(v, "D", (0,))
-    for role in "BMD":
-        ask(role)
-    pack_columns("D")
-    for q in (v, sc):
-        q.wait_ge(S.l_w, 32)
-    for role in "BMD":
-        expert(v, role, 0, CUT)
-        expert(sc, role, CUT, 512)
-        pack_expert(role)
-    v.wait_ge(S.l_po, 64)
-    v.tensor_scalar(T.oa[:], T.po[:, 32:64], float(ALL), None, A.mult).then_inc(S.e_oa, 1)
-    if not OWN_BY_DMA:
-        expert(v, "O", 0, CUT)
-        expert(sc, "O", CUT, 512)
-    v.wait_ge(S.e_oa, 1)
-    v.tensor_tensor(T.ob[:], T.oa[:], T.po[:, 0:32], A.add).then_inc(S.e_ob, 1)
-    pack_expert("O")
-    columns(sc, "O", (1, 2, 3))
-    columns(v, "O", (0,))
-    v.wait_ge(S.e_ob, 1)
-    for k in range(4):
-        v.tensor_copy(T.off[32 * k:32 * k + 32, :], T.ob[:]).then_inc(S.e_off, 1)
-    pack_columns("O")
+        q.wait_ge(S.l_x, 16 * len(XCUTS))
+    do = {"columns": columns, "pack_columns": pack_columns, "ask": ask, "expert": expert, "pack_expert": pack_expert,
+          "pack_both": pack_both, "places": places}
+    for step in STEPS:
+        do[step[0]](*step[1:])
 
     def have(kind, role):
         if role == "O":
-            return [(S["q" + kind + "O"], 1)]
+            return [(S.both if kind == "e" and role in BOTH else S["q" + kind + "O"], 1)]
         return [arrives(kind + "c", role, r, T, topo), arrives(kind + "p", role, r, T, topo)]
-    mine, far = r // 2, 1 - r // 2
-    by_rank = {d: q for q, d in R.items()}
-    order = [("O", far), ("O", mine), ("M", far), ("M", mine), ("D", far), ("D", mine), ("B", far), ("B", mine)]
     seen = []
-    for k, (role, pair) in enumerate(order):
-        for need in [("e", role), ("x", by_rank[2 * pair]), ("x", by_rank[2 * pair + 1])]:
+    for k, (role, m, who) in enumerate(ORDER):
+        for need in [("e", role)] + [("x", q) for q in who]:
             if need not in seen:
                 seen.append(need)
                 for sem, val in have(*need):
                     te.wait_ge(sem, val)
-        e, a = R[role], pair * PAIR
-        bank = T.ps[:, 512 * k:512 * k + PAIR]
-        te.matmul_mx(bank, T.ec[:, e * F:(e + 1) * F], T.ep[:, e * F:(e + 1) * F],
-                     T.xc[:, a:a + PAIR], T.xp[:, a:a + PAIR], True, True).then_inc(S["mm%d" % k], 1)
-        q = sc if k % 2 == 0 else v
+        if k >= BANKS:
+            te.wait_ge(S["cp%d" % (k - BANKS)], 1)
+        e, (a, z) = place_of(R[role], r, T, topo) + m, slots(who)
+        W, Wp, b = (T.bec, T.bep, m) if role == "O" and role in BOTH else (T.ec, T.ep, e)
+        bank = T.ps[:, 512 * (k % BANKS):512 * (k % BANKS) + z - a]
+        te.matmul_mx(bank, W[:, b * F:(b + 1) * F], Wp[:, b * F:(b + 1) * F],
+                     T.xc[:, a:z], T.xp[:, a:z], True, True).then_inc(S["mm%d" % k], 1)
+        q = sc if COPIERS[k] == "s" else v
         q.wait_ge(S["mm%d" % k], 1)
-        o = T.res[:, e * ALL + a:e * ALL + a + PAIR]
+        o = T.res[:, e * ALL + a:e * ALL + z]
+        done = S["cp%d" % k] if k + BANKS < len(ORDER) else S.cp
         if q is sc:
-            sc.activation(o, bank, COPY).then_inc(S.cp, 1)
+            sc.activation(o, bank, COPY).then_inc(done, 1)
         else:
-            v.tensor_copy(o, bank).then_inc(S.cp, 1)
+            v.tensor_copy(o, bank).then_inc(done, 1)
 
     for q in (v, sc):
-        q.wait_ge(S.e_off, 4)
-        q.wait_ge(S.cp, len(order))
-    for k, q in enumerate((v, sc)):
-        pick(q, T.yb[:, 256 * k:256 * k + 256], T.res[:], T.off[:, 16 * k:16 * k + 16], S["y%d" % k])
-    for k, q in enumerate((sy, sc)):
+        q.wait_ge(S.e_off, 2)
+        for k in range(len(ORDER) - BANKS):
+            q.wait_ge(S["cp%d" % k], 1)
+        q.wait_ge(S.cp, min(len(ORDER), BANKS))
+    pieces = ((v, sy, 0, 128), (sc, sc, 256, 512), (v, sy, 128, 256))
+    for k, (q, _, a, b) in enumerate(pieces):
+        pick(q, T.yb[:, a:b], T.res[:], T.off[:, a // 16:b // 16], S["y%d" % k])
+    for k, (_, q, a, b) in enumerate(pieces):
         q.wait_ge(S["y%d" % k], 1)
-        q.dma_start(T.y[:, 256 * k:256 * k + 256], T.yb[:, 256 * k:256 * k + 256]).then_inc(S.st, 16)
-    sy.wait_ge(S.st, 32)
+        q.dma_start(T.y[:, a:b], T.yb[:, a:b]).then_inc(S.st, 16)
+    sy.wait_ge(S.st, 16 * len(pieces))

from concourse.bass import DstId, RemoteDMATransfer
from concourse.mybir import dt, AluOpType, ActivationFunctionType

N, COLS, CAP, F = 4, 512, 192, 128
NCORES = 112
PAIR = 2 * CAP
ALL = N * CAP
CODES = "float8_e4m3fn_x4"
ROLES = "MBD"
BOTH = ""
EXPERTS = N + len(BOTH)
XCUTS = ((0, 16), (16, 48), (48, 80), (80, 128))

SCRATCH = {
    "xs": ("sbuf", [128, 4 * COLS], "bfloat16"),
    "ws": ("sbuf", [128, 8 * F], "bfloat16"),
    "slist": ("sbuf", [32, ALL // 16], "int32"),
    "seli": ("sbuf", [128, 16], "int32"),
    "po": ("sbuf", [64, 64], "int32"),
    "ip": ("sbuf", [128, 32], "int32"),
    "ia": ("sbuf", [128, 32], "int32"),
    "ic": ("sbuf", [128, 32], "int32"),
    "jj": ("sbuf", [128, 32], "float32"),
    "junk": ("sbuf", [128, 512], "float32"),
    "self_": ("sbuf", [128, 16], "float32"),
    "selb": ("sbuf", [128, 4], "float32"),
    "selin": ("sbuf", [128, 4], "float32"),
    "ox": ("sbuf", [128, ALL // 16], "uint16"),
    "oe": ("sbuf", [128, 32 * N], "uint16"),
    "edge": ("sbuf", [64, 4], "float32"),
    "oa": ("sbuf", [64, 32 * 12], "float32"),
    "off": ("sbuf", [128, 32], "uint16"),
    "xt": ("sbuf", [128, 4 * ALL], "bfloat16"),
    "et": ("sbuf", [128, 4 * F * N], "bfloat16"),
    "oxc": ("sbuf", [128, ALL], CODES),
    "oxp": ("sbuf", [128, ALL], "uint8"),
    "oec": ("sbuf", [128, N * F], CODES),
    "oep": ("sbuf", [128, N * F], "uint8"),
    "bec": ("sbuf", [128, 2 * F], CODES),
    "bep": ("sbuf", [128, 2 * F], "uint8"),
    "xc": ("sbuf", [128, ALL], CODES),
    "xp": ("sbuf", [128, ALL], "uint8"),
    "ec": ("sbuf", [128, EXPERTS * F], CODES),
    "ep": ("sbuf", [128, EXPERTS * F], "uint8"),
    "ps": ("psum", [128, 4096], "float32"),
    "res": ("sbuf", [128, EXPERTS * ALL], "float32"),
    "yb": ("sbuf", [128, COLS], "float32"),
}

CALLS = [
    (["e_selb"], [("sel", "B", "straight", 0, 8)]),
    ([], [("sel", "M", "straight", 0, 8)]),
    ([], [("sel", "D", "straight", 0, 8)]),
    (["qxM"], [("xp", "M", "mate", 0, 8), ("xp", "B", "die", 8, 16)]),
    ([], [("xc", "M", "mate", 0, 8), ("xc", "B", "die", 8, 16)]),
    (["qxD"], [("xc", "D", "straight", 0, 8)]),
    ([], [("xp", "D", "straight", 0, 8)]),
    (["qeB"], [("ec", "B", "die", 8, 16)]),
    (["qeM"], [("ec", "M", "straight", 0, 8)]),
    ([], [("ep", "M", "straight", 0, 4), ("ep", "B", "straight", 4, 8)]),
    (["qeD"], [("ec", "D", "straight", 0, 8)]),
    ([], [("ep", "D", "straight", 0, 8)]),
]
STEPS = [("columns", "MB", 768), ("pack_columns", "MB"),
         ("columns", "D", 192), ("ask", "B"), ("pack_columns", "D"), ("ask", "M"),
         ("expert", "B", 192), ("ask", "D"), ("pack_expert", "B"), ("expert", "M", 192), ("pack_expert", "M"),
         ("expert", "D", 192), ("pack_expert", "D"), ("expert", "O", 0), ("places", 0),
         ("columns", "O", 384), ("places", 1), ("pack_expert", "O"), ("places", 2), ("pack_columns", "O")]
COPIERS = "svsvsvsvsv"
ORDER = [("O", 0, "OD"), ("O", 0, "MB"), ("M", 0, "OD"), ("M", 0, "MB"), ("B", 0, "OD"), ("B", 0, "MB"),
         ("D", 0, "M"), ("D", 0, "B"), ("D", 0, "O"), ("D", 0, "D")]
BANKS = 8

SEMAPHORES = (["l_sel", "l_list", "l_w", "l_x", "l_po", "e_i1", "e_i2", "e_ia", "e_j", "e_self", "e_selb", "e_ox",
               "e_edge", "e_off", "both", "sent", "cp", "y0", "y1", "y2", "y3", "st"]
              + [k + q for k in ("sel", "xc", "xp", "ec", "ep") for q in ROLES]
              + [k + q for k in ("gx", "qx", "oe", "ge", "qe") for q in ROLES + "O"]
              + ["oa%d" % k for k in range(6)] + ["mm%d" % k for k in range(len(ORDER))]
              + ["cp%d" % k for k in range(len(ORDER) - BANKS)])


def u8(view):
    return view.bitcast(dt.uint8)


def bits(engines):
    return sum(1 << e for e in engines)


def roles(r, T, topo):
    chip = [topo.chip(c) for c in T.cores]
    mine = [d for d in range(N) if d == r or topo.same_plane(chip[d], chip[r])]
    other = [d for d in range(N) if d not in mine]
    i = mine.index(r)
    return {"O": r, "B": mine[1 - i], "D": other[i], "M": other[1 - i]}


def helper(s, role, way, T, topo):
    c, dst = T.cores[s], T.cores[roles(s, T, topo)[role]]
    if way == "mate":
        ks = [k for k in range(NCORES) if topo.mates(topo.chip(k), topo.chip(dst)) and topo.die(k) == topo.die(c)
              and topo.may_write(k, dst) and topo.may_write(c, k)]
        return ks[0]
    near = way == "near"
    ks = [k for k in topo.cores_of(c) if k != c and (topo.die(k) == topo.die(c)) == near and topo.may_write(k, dst)]
    if role == "B":
        far = T.cores[roles(s, T, topo)["D"]]
        return [k for k in ks if not topo.may_write(k, far)][0]
    return ks["DM".index(role) % len(ks)]


def place_of(h, r, T, topo):
    R = roles(r, T, topo)
    return h + sum(R[q] < h for q in BOTH)


def landing(kind, s, role, T, topo):
    if kind == "sel":
        return T.selin[:, s:s + 1]
    if kind[0] == "x":
        view = T[kind][:, s * CAP:(s + 1) * CAP]
    else:
        e = place_of(s, roles(s, T, topo)[role], T, topo)
        view = T[kind][:, e * F:(e + 1 + (role in BOTH)) * F]
    return u8(view) if kind[1] == "c" else view


def leaving(kind, s, role, T, topo):
    d = roles(s, T, topo)[role]
    if kind == "sel":
        return T.selb[:, d:d + 1]
    if kind[0] == "e" and role in BOTH:
        view = T["b" + kind][:]
    else:
        w = CAP if kind[0] == "x" else F
        view = T["o" + kind][:, d * w:(d + 1) * w]
    return u8(view) if kind[1] == "c" else view


def arrives(kind, role, r, T, topo):
    for _, items in CALLS:
        for k, q, way, a, b in items:
            if (k, q) == (kind, role):
                s = roles(r, T, topo)[role]
                n = b - a if way == "straight" else len(topo.engines(helper(s, role, way, T, topo), T.cores[r]))
                return T.sem[kind + role], n


def hand_on(g, core, T, topo):
    sent = 0
    for _, items in CALLS:
        for kind, role, way, a, b in items:
            for s in range(N):
                if way != "straight" and helper(s, role, way, T, topo) == core:
                    dst = T.cores[roles(s, T, topo)[role]]
                    rid, pid, _ = topo.addr(dst)
                    view = landing(kind, s, role, T, topo)
                    g.wait_ge(T.sem[kind + role], b - a)
                    g.remote_dma(view, view, T.sem[kind + role], T.sem.sent, pid, rid, topo.mask(core, dst))
                    sent += len(topo.engines(core, dst))
    if sent:
        g.wait_ge(T.sem.sent, sent)


def rank_program(g, core, T, topo):
    r = T.rank_of(core)
    if r is None:
        hand_on(g, core, T, topo)
        return
    S, v, sc, te, sy = T.sem, g.vector, g.scalar, g.tensor, g.sync
    A, COPY = AluOpType, ActivationFunctionType.Copy
    R = roles(r, T, topo)

    sc.dma_start(T.seli[0:1, 0:16], T.sel[:]).then_inc(S.l_sel, 16)
    sc.dma_start(T.slist[16:32, :], T.send[:]).then_inc(S.l_list, 16)
    sc.dma_start(T.slist[0:16, :], T.send[:]).then_inc(S.l_list, 16)
    for a, b in XCUTS:
        sy.dma_start(T.xs[a:b, :], T.x[a:b, :]).then_inc(S.l_x, 16)
    sy.dma_start(T.ws[:, 0:512], T.w[0:128, :]).then_inc(S.l_w, 16)
    sy.dma_start(T.ws[:, 512:1024], T.w[128:256, :]).then_inc(S.l_w, 16)
    for k in range(4):
        sy.dma_start(T.po[16 * k:16 * k + 16, 0:32], T.place[:]).then_inc(S.l_po, 16)
        sy.dma_start(T.po[16 * k:16 * k + 16, 32:64], T.of[:]).then_inc(S.l_po, 16)

    g.iota(T.ip[:], [[0, 32]], 0, 1).then_inc(S.e_i1, 1)
    g.iota(T.ic[:], [[16, 32]], 0, 0).then_inc(S.e_i2, 1)
    g.wait_ge(S.e_self, 1)
    g.partition_broadcast(T.selb[:, 0:4], T.self_[0:1, 0:4], 128).then_inc(S.e_selb, 1)
    sent = 0
    for waits, items in CALLS:
        for name in waits:
            g.wait_ge(S[name], 1)
        tr = []
        for kind, role, way, a, b in items:
            dst = T.cores[R[role]] if way == "straight" else helper(r, role, way, T, topo)
            rid, pid, _ = topo.addr(dst)
            tr.append(RemoteDMATransfer(dst_ids=[DstId(rid=rid, pnc=pid)], dma_engine_mask=bits(topo.engines(core, dst)[a:b]),
                                        remote_sem=S[kind + role], src=leaving(kind, r, role, T, topo),
                                        dst=landing(kind, r, role, T, topo)))
            sent += b - a
        g.remote_dma_fused(tr, local_sem=S.sent)
    g.wait_ge(S.sent, sent)

    def pick(q, out, window, offsets, sem):
        if q is v:
            v.tensor_copy(out, window.indirect(offsets)).then_inc(sem, 1)
        else:
            sc.activation(out, window.indirect(offsets), COPY).then_inc(sem, 1)

    def slots(who):
        ds = sorted(R[q] for q in who)
        assert ds[-1] - ds[0] == len(ds) - 1
        return ds[0] * CAP, (ds[-1] + 1) * CAP

    calls = {}
    have_w = []

    def need_w(q):
        if q not in have_w:
            have_w.append(q)
            (v if q == "v" else sc).wait_ge(S.l_w, 32)

    def columns(who, share):
        a, b = slots(who)
        calls["x" + who] = 0
        for t in range(4):
            cut = a + min(b - a, max(0, share - t * (b - a)))
            for q, lo, hi in ((v, a, cut), (sc, cut, b)):
                if hi > lo:
                    pick(q, T.xt[:, 4 * lo + t:4 * hi:4], T.xs[:, t:4 * COLS], T.ox[:, lo // 16:hi // 16], S["gx" + who[0]])
                    calls["x" + who] += 1

    def pack_columns(who):
        a, b = slots(who)
        c, p = (T.xc, T.xp) if who == "O" else (T.oxc, T.oxp)
        v.wait_ge(S["gx" + who[0]], calls["x" + who])
        v.quantize_mx(c[:, a:b], p[:, a:b], T.xt[:, 4 * a:4 * b]).then_inc(S["qx" + who[0]], 1)

    def ask(role):
        d = R[role]
        if role == "O":
            v.wait_ge(S.e_selb, 1)
            col = T.selb[:, d:d + 1]
        else:
            v.wait_ge(*arrives("sel", role, r, T, topo))
            col = T.selin[:, d:d + 1]
        v.tensor_scalar(T.oe[:, 32 * d:32 * d + 32], T.jj[:], col, None, A.add).then_inc(S["oe" + role], 1)

    def expert(role, share, now="vs"):
        d = R[role]
        calls.setdefault("e" + role, 0)
        for name, q, a, b in (("v", v, 0, share), ("s", sc, share, 4 * F)):
            if b > a and name in now:
                need_w(name)
                q.wait_ge(S["oe" + role], 1)
                pick(q, T.et[:, 512 * d + a:512 * d + b], T.ws[:], T.oe[:, 32 * d + a // 16:32 * d + b // 16], S["ge" + role])
                calls["e" + role] += 1

    def pack_expert(role):
        d = R[role]
        e, c, p = (place_of(d, r, T, topo), T.ec, T.ep) if role == "O" else (d, T.oec, T.oep)
        v.wait_ge(S["ge" + role], calls["e" + role])
        v.quantize_mx(c[:, e * F:(e + 1) * F], p[:, e * F:(e + 1) * F], T.et[:, 512 * d:512 * (d + 1)]).then_inc(S["qe" + role], 1)

    def pack_both():
        need_w("v")
        v.quantize_mx(T.bec[:], T.bep[:], T.ws[:]).then_inc(S.both, 1)

    def places(step):
        part = [T.oa[:, 32 * k:32 * k + 32] for k in range(12)]
        n = len(BOTH)
        if step == 0:
            v.wait_ge(S.l_po, 128)
            v.tensor_scalar(part[0], T.po[:, 32:64], float(ALL), None, A.mult).then_inc(S.oa0, 1)
            if n:
                v.wait_ge(S.e_edge, n)
            for k in range(n):
                v.tensor_scalar(part[1 + k], T.po[:, 32:64], T.edge[:, k:k + 1], float(ALL), A.is_ge, A.mult).then_inc(S.oa0, 1)
            return
        if step == 1:
            v.wait_ge(S.oa0, 1 + n)
            v.tensor_tensor(part[6], part[0], T.po[:, 0:32], A.add).then_inc(S.oa1, 1)
            return
        for k in range(n):
            v.wait_ge(S["oa%d" % (1 + k)], 1)
            v.tensor_tensor(part[7 + k], part[6 + k], part[1 + k], A.add).then_inc(S["oa%d" % (2 + k)], 1)
        v.wait_ge(S["oa%d" % (1 + n)], 1)
        for k in range(2):
            v.tensor_copy(T.off[64 * k:64 * k + 64, :], part[6 + n]).then_inc(S.e_off, 1)

    v.wait_ge(S.e_i1, 1)
    v.tensor_scalar(T.ia[:], T.ip[:], 15, None, A.bitwise_and).then_inc(S.e_ia, 1)
    v.wait_ge(S.e_i2, 1)
    v.wait_ge(S.e_ia, 1)
    v.tensor_tensor(T.jj[:], T.ia[:], T.ic[:], A.add).then_inc(S.e_j, 1)
    v.wait_ge(S.l_sel, 16)
    v.tensor_scalar(T.self_[0:1, :], T.seli[0:1, :], 512.0, 0.0, A.mult, A.max).then_inc(S.e_self, 1)
    v.wait_ge(S.l_list, 32)
    for k in range(4):
        v.tensor_scalar(T.ox[32 * k:32 * k + 32, :], T.slist[:], 4.0, 0.0, A.mult, A.max).then_inc(S.e_ox, 1)
    v.wait_ge(S.e_j, 1)
    v.wait_ge(S.e_selb, 1)
    if "O" not in BOTH:
        ask("O")
    for k, role in enumerate(BOTH):
        d = R[role]
        v.tensor_scalar(T.edge[:, k:k + 1], T.selb[0:64, d:d + 1], -1 / 512.0, d + 1.0, A.mult, A.add).then_inc(S.e_edge, 1)
    for q in (v, sc):
        q.wait_ge(S.e_ox, 4)
        q.wait_ge(S.l_x, 16 * len(XCUTS))
    do = {"columns": columns, "pack_columns": pack_columns, "ask": ask, "expert": expert, "pack_expert": pack_expert,
          "pack_both": pack_both, "places": places}
    for step in STEPS:
        do[step[0]](*step[1:])

    def have(kind, role):
        if role == "O":
            return [(S.both if kind == "e" and role in BOTH else S["q" + kind + "O"], 1)]
        return [arrives(kind + "c", role, r, T, topo), arrives(kind + "p", role, r, T, topo)]
    seen = []
    for k, (role, m, who) in enumerate(ORDER):
        for need in [("e", role)] + [("x", q) for q in who]:
            if need not in seen:
                seen.append(need)
                for sem, val in have(*need):
                    te.wait_ge(sem, val)
        if k >= BANKS:
            te.wait_ge(S["cp%d" % (k - BANKS)], 1)
        e, (a, z) = place_of(R[role], r, T, topo) + m, slots(who)
        W, Wp, b = (T.bec, T.bep, m) if role == "O" and role in BOTH else (T.ec, T.ep, e)
        bank = T.ps[:, 512 * (k % BANKS):512 * (k % BANKS) + z - a]
        te.matmul_mx(bank, W[:, b * F:(b + 1) * F], Wp[:, b * F:(b + 1) * F],
                     T.xc[:, a:z], T.xp[:, a:z], True, True).then_inc(S["mm%d" % k], 1)
        q = sc if COPIERS[k] == "s" else v
        q.wait_ge(S["mm%d" % k], 1)
        o = T.res[:, e * ALL + a:e * ALL + z]
        done = S["cp%d" % k] if k + BANKS < len(ORDER) else S.cp
        if q is sc:
            sc.activation(o, bank, COPY).then_inc(done, 1)
        else:
            v.tensor_copy(o, bank).then_inc(done, 1)

    for q in (v, sc):
        q.wait_ge(S.e_off, 2)
        for k in range(len(ORDER) - BANKS):
            q.wait_ge(S["cp%d" % k], 1)
        q.wait_ge(S.cp, min(len(ORDER), BANKS))
    pieces = ((v, sy, 0, 128), (sc, sc, 256, 512), (v, sy, 128, 256))
    for k, (q, _, a, b) in enumerate(pieces):
        pick(q, T.yb[:, a:b], T.res[:], T.off[:, a // 16:b // 16], S["y%d" % k])
    for k, (_, q, a, b) in enumerate(pieces):
        q.wait_ge(S["y%d" % k], 1)
        q.dma_start(T.y[:, a:b], T.yb[:, a:b]).then_inc(S.st, 16)
    sy.wait_ge(S.st, 16 * len(pieces))
